import numpy as np
import ml_dtypes


def mxq(x, axis, fmt="e4m3"):
    dtype, down = {"e4m3": (ml_dtypes.float8_e4m3fn, 7), "e5m2": (ml_dtypes.float8_e5m2, 14)}[fmt]
    v = np.moveaxis(np.asarray(x, np.float32).astype(ml_dtypes.bfloat16).astype(np.float64), axis, -1)
    blocks = v.reshape(v.shape[:-1] + (-1, 32))
    amax = np.abs(blocks).max(-1, keepdims=True)
    byte = np.maximum(np.where(amax > 0, np.frexp(amax)[1] - 1 + 127, 0) - down, 1)
    scale = np.exp2(byte - 127.0)
    codes = (blocks / scale).astype(np.float32).astype(dtype).astype(np.float64)
    return np.moveaxis((codes * scale).reshape(v.shape), -1, axis)


WIDE = False


def mx_kscale(k):
    if not WIDE:
        return np.ones(k)
    levels = np.array([10, -10, 5, -5, 0])
    if k % 512:
        return np.exp2(np.random.permutation(np.resize(levels, k // 32))).repeat(32)
    a = np.empty((k // 512, 16))
    for p in range(k // 512):
        a[p, :8] = np.random.permutation(np.resize(levels, 8))
        for g in range(8):
            far = levels[np.abs(levels - a[p, g]) >= 10]
            a[p, g + 8] = far[np.random.randint(len(far))]
    return np.exp2(a.ravel()).repeat(32)


def f64(x):
    return np.asarray(x).astype(np.float64)


def striped(idx):
    return np.tile(idx.reshape(-1, 16).T, (8, 1)).astype(np.uint16)


def unstriped(offs):
    return offs[:16].T.reshape(-1).astype(np.int64)


def pack_weight(w):
    k, n = w.shape
    w = f64(np.asarray(w, np.float32).astype(ml_dtypes.bfloat16)).reshape(k // 32, 32, n)
    amax = np.abs(w).max(1)
    byte = np.clip(np.where(amax > 0, np.frexp(amax)[1] - 1 + 127 - 7, 1), 1, 254)
    scaled = (w * np.exp2(127.0 - byte)[:, None, :]).reshape(k, n).astype(np.float32)
    words = np.ascontiguousarray(scaled.reshape(k // 512, 128, 4, n).transpose(0, 1, 3, 2)).astype(ml_dtypes.float8_e4m3fn).view(np.uint8)
    return words, np.ascontiguousarray(byte.astype(np.uint8).reshape(k // 512, 16, n))


def unpack_weight(words, scales):
    g, p, n, _ = words.shape
    vals = np.ascontiguousarray(words).view(ml_dtypes.float8_e4m3fn).astype(np.float64) * np.repeat(np.exp2(scales.astype(np.float64) - 127.0), 8, axis=1)[..., None]
    return vals.transpose(0, 1, 3, 2).reshape(g * 512, n)


def relu(v):
    return np.maximum(v, 0.0)


K, T, H, N = 1024, 512, 512, 256


def setup_inputs():
    n = np.random.standard_normal
    s = mx_kscale(K)[:, None]
    u = mx_kscale(H)
    packed_xT = pack_weight(n((K, T)) * s)
    packed_w2 = pack_weight(n((H, N)) / np.sqrt(2 * H) / u[:, None])
    packed_w3 = pack_weight(n((H, N)) / np.sqrt(2 * H) / u[:, None])
    return {
        "x_words": packed_xT[0],
        "x_scales": packed_xT[1],
        "w1": (n((K, H)) / np.sqrt(K) / s * u).astype(np.float32),
        "w2_words": packed_w2[0],
        "w2_scales": packed_w2[1],
        "w3_words": packed_w3[0],
        "w3_scales": packed_w3[1],
        "pos1": striped(np.random.permutation(T)),
        "pos2": striped(np.random.permutation(T)),
        "pos3": striped(np.random.permutation(T)),
    }


def reference(x_words, x_scales, w1, w2_words, w2_scales, w3_words, w3_scales, pos1, pos2, pos3):
    xq = unpack_weight(x_words, x_scales)
    h = relu(mxq(f64(w1), 0, "e4m3").T @ xq)
    z = np.maximum(np.maximum(h[:, unstriped(pos1)], h[:, unstriped(pos2)]), h[:, unstriped(pos3)])
    return unpack_weight(w2_words, w2_scales).T @ mxq(h, 0, "e4m3") + unpack_weight(w3_words, w3_scales).T @ mxq(z, 0, "e4m3")

@@ -1,0 +1,223 @@
+from contextlib import ExitStack
+
+import concourse.mybir as mybir
+
+K, T, H, N = 1024, 512, 512, 256
+FLOPS = 2 * K * H * T + 2 * 2 * H * N * T
+
+F32 = mybir.dt.float32
+BF16 = mybir.dt.bfloat16
+I32 = mybir.dt.int32
+U32 = mybir.dt.uint32
+U16 = mybir.dt.uint16
+U8 = mybir.dt.uint8
+FP8X4 = mybir.dt.float8_e4m3fn_x4
+MAX = mybir.AluOpType.max
+RELU = mybir.ActivationFunctionType.Relu
+
+P = 128
+PACK = 4
+HEAD = 384
+TAIL = T - HEAD
+WINDOW = 2 * HEAD
+M_VECTOR = 88
+
+
+def tile_picked_wsagecat_max_l_kernel(
+    tc, x_words, x_scales, w1, w2_words, w2_scales, w3_words, w3_scales, pos1, pos2, pos3, out
+):
+    nc = tc.nc
+    with ExitStack() as ctx:
+        lists_pool = ctx.enter_context(tc.tile_pool(name="lists", bufs=1))
+        keep = ctx.enter_context(tc.tile_pool(name="keep", bufs=1))
+        psum = ctx.enter_context(tc.psum_pool(name="psum", bufs=1))
+
+        def sbuf(shape, dtype, name, tag=None):
+            return keep.tile(shape, dtype, name=name, tag=tag or name, align_bytes=64)
+
+        x_plane = sbuf([P, T], U8, "x_plane")
+        w_plane = sbuf([P, 2, N], U8, "w_plane")
+        nc.vector.memset(x_plane[:].bitcast(I32), 0)
+
+        w1_rows = w1.rearrange("(g p j) c -> g p j c", g=2, j=PACK)
+        raw0 = sbuf([P, PACK, H], F32, "raw0")
+        raw1 = [sbuf([P, 2, H], F32, "raw1_%d" % u) for u in range(2)]
+        nc.sync.dma_start(out=raw0[:], in_=w1_rows[0])
+        for q in range(4):
+            nc.sync.dma_start(
+                out=x_plane[32 * q : 32 * q + 8, :].bitcast(I32),
+                in_=x_scales[:, 4 * q : 4 * q + 4, :].bitcast(I32),
+            )
+        for u in range(2):
+            nc.sync.dma_start(out=raw1[u][:], in_=w1_rows[1][:, 2 * u : 2 * u + 2, :])
+        x_codes = [sbuf([P, T], U32, "x_codes%d" % g) for g in range(2)]
+        for g in range(2):
+            nc.sync.dma_start(
+                out=x_codes[g][:].bitcast(I32), in_=x_words[g].rearrange("p n r -> p (n r)").bitcast(I32)
+            )
+        lists = []
+        for d, pos in enumerate((pos1, pos2, pos3)):
+            offsets = lists_pool.tile([P, T // 16], U16, name="offsets%d" % d)
+            nc.sync.dma_start(offsets[:], pos)
+            lists.append(offsets)
+        w_codes = []
+        for i, words in enumerate((w2_words, w3_words)):
+            codes = sbuf([P, N], U32, "w_codes%d" % i)
+            nc.sync.dma_start(
+                out=codes[:].bitcast(I32), in_=words[0].rearrange("p n r -> p (n r)").bitcast(I32)
+            )
+            w_codes.append(codes)
+        nc.vector.memset(w_plane[:].rearrange("p i n -> p (i n)").bitcast(I32), 0)
+        for i, scales in enumerate((w2_scales, w3_scales)):
+            for q in range(4):
+                nc.sync.dma_start(
+                    out=w_plane[32 * q : 32 * q + 4, i, :].bitcast(I32),
+                    in_=scales[0, 4 * q : 4 * q + 4, :].bitcast(I32),
+                )
+
+        windows = [sbuf([P, WINDOW], F32, "window%d" % t) for t in range(PACK)]
+        for t in range(PACK):
+            nc.vector.memset(windows[t][:, T:], 0.0)
+
+        w1_bf = [sbuf([P, PACK, P, PACK], BF16, "w1_bf%d" % g) for g in range(2)]
+        w1_codes = [sbuf([P, H], U32, "w1_codes%d" % g) for g in range(2)]
+        w1_plane = [sbuf([P, H], U8, "w1_plane%d" % g) for g in range(2)]
+
+        def cast(dst, src):
+            dst = dst.rearrange("p t m j -> p m j t")
+            src = src.rearrange("p j (m t) -> p m j t", t=PACK)
+            nc.vector.tensor_copy(out=dst[:, :M_VECTOR], in_=src[:, :M_VECTOR])
+            nc.scalar.copy(out=dst[:, M_VECTOR:], in_=src[:, M_VECTOR:])
+
+        def quantise_w1(g, t0, t1):
+            nc.vector.quantize_mx(
+                out=w1_codes[g][:, P * t0 : P * t1].bitcast(FP8X4),
+                scales=w1_plane[g][:, P * t0 : P * t1],
+                in_=w1_bf[g][:, t0:t1].rearrange("p t m j -> p (t m j)"),
+            )
+
+        cast(w1_bf[0][:], raw0[:])
+        quantise_w1(0, 0, 4)
+        for u in range(2):
+            cast(w1_bf[1][:, :, :, 2 * u : 2 * u + 2], raw1[u][:])
+        quantise_w1(1, 0, 1)
+        quantise_w1(1, 1, 2)
+        quantise_w1(1, 2, 4)
+
+        banks = [psum.tile([P, T], F32, name="h_bank%d" % t) for t in range(PACK)]
+        for t in range(PACK):
+            cols = slice(P * t, P * (t + 1))
+            for g in range(2):
+                nc.tensor.matmul_mx(
+                    out=banks[t][:],
+                    lhsT=w1_codes[g][:, cols].bitcast(FP8X4),
+                    lhsT_scale=w1_plane[g][:, cols],
+                    rhs=x_codes[g][:].bitcast(FP8X4),
+                    rhs_scale=x_plane[4 * g :, :],
+                    start=(g == 0),
+                    stop=(g == 1),
+                )
+            nc.scalar.activation(out=windows[t][:, :T], in_=banks[t][:], func=RELU)
+
+        def interleave(dst, src):
+            nc.scalar.copy(
+                out=dst.rearrange("p (c i) t -> p c t i", i=4),
+                in_=src.rearrange("p t (c i) -> p c t i", i=4),
+            )
+
+        h_rows = sbuf([P, PACK, T], BF16, "h_rows")
+        for t in range(PACK):
+            nc.scalar.activation(out=h_rows[:, t, :], in_=banks[t][:], func=RELU)
+        h_words = sbuf([P, T, PACK], BF16, "h_words", tag="reuse_h")
+        interleave(h_words[:], h_rows[:])
+
+        def gather(dst, t, d, v0, v1):
+            nc.vector.tensor_copy(out=dst, in_=windows[t][:].indirect(lists[d][:, v0 // 16 : v1 // 16]))
+
+        def quantise(codes, plane, words):
+            nc.vector.quantize_mx(
+                out=codes.bitcast(FP8X4), scales=plane, in_=words.rearrange("p v t -> p (v t)")
+            )
+
+        picked = [sbuf([P, PACK, HEAD], BF16, "picked%d" % d) for d in range(3)]
+        z_rows = sbuf([P, PACK, HEAD], BF16, "z_rows")
+
+        def first_max(ts):
+            nc.vector.tensor_tensor(out=z_rows[:, ts], in0=picked[0][:, ts], in1=picked[1][:, ts], op=MAX)
+
+        def second_max(ts):
+            nc.vector.tensor_tensor(out=z_rows[:, ts], in0=z_rows[:, ts], in1=picked[2][:, ts], op=MAX)
+
+        for t in range(2):
+            for d in range(3):
+                gather(picked[d][:, t, :], t, d, 0, HEAD)
+        gather(picked[0][:, 2, :], 2, 0, 0, HEAD)
+        first_max(slice(0, 2))
+        gather(picked[1][:, 2, :], 2, 1, 0, HEAD)
+        second_max(slice(0, 2))
+        gather(picked[2][:, 2, :], 2, 2, 0, HEAD)
+        for d in range(3):
+            gather(picked[d][:, 3, :], 3, d, 0, HEAD)
+        first_max(slice(2, 4))
+        h_codes = sbuf([P, T], U32, "h_codes")
+        h_plane = sbuf([P, T], U8, "h_plane")
+        quantise(h_codes[:], h_plane[:], h_words[:])
+        second_max(slice(2, 4))
+        z_words = sbuf([P, HEAD, PACK], BF16, "z_words", tag="reuse_z")
+        interleave(z_words[:], z_rows[:])
+
+        late0 = sbuf([P, PACK, TAIL], BF16, "late0", tag="reuse_h")
+        late1 = sbuf([P, PACK, TAIL], BF16, "late1")
+        for d, dst in enumerate((late0, late1)):
+            for t in range(PACK):
+                gather(dst[:, t, :], t, d, HEAD, T)
+        z_codes = sbuf([P, HEAD], U32, "z_codes")
+        z_plane = sbuf([P, HEAD], U8, "z_plane")
+        quantise(z_codes[:, :256], z_plane[:, :256], z_words[:, :256, :])
+        pair_rows = sbuf([P, PACK, TAIL], BF16, "pair_rows")
+        nc.vector.tensor_tensor(out=pair_rows[:], in0=late0[:], in1=late1[:], op=MAX)
+        quantise(z_codes[:, 256:], z_plane[:, 256:], z_words[:, 256:, :])
+        pair_words = sbuf([P, TAIL, PACK], BF16, "pair_words")
+        interleave(pair_words[:], pair_rows[:])
+        late2 = sbuf([P, PACK, TAIL], BF16, "late2", tag="reuse_z")
+        for t in range(PACK):
+            gather(late2[:, t, :], t, 2, HEAD, T)
+
+        def product(bank, m, i, codes, plane):
+            cols = slice(P * m, P * (m + 1))
+            nc.tensor.matmul_mx(
+                out=bank,
+                lhsT=w_codes[i][:, cols].bitcast(FP8X4),
+                lhsT_scale=w_plane[:, i, cols],
+                rhs=codes.bitcast(FP8X4),
+                rhs_scale=plane,
+                start=(i == 0),
+                stop=(i == 1),
+            )
+
+        out_rows = out.rearrange("(m p) v -> p m v", p=P)
+        tail_banks = [psum.tile([P, TAIL], F32, name="tail_bank%d" % m) for m in range(2)]
+        for m in range(2):
+            product(tail_banks[m][:], m, 0, h_codes[:, HEAD:], h_plane[:, HEAD:])
+        head_result = sbuf([P, 2, HEAD], F32, "head_result")
+        for m in range(2):
+            bank = psum.tile([P, HEAD], F32, name="head_bank%d" % m)
+            for cols in (slice(0, 256), slice(256, HEAD)):
+                product(bank[:, cols], m, 0, h_codes[:, cols], h_plane[:, cols])
+                product(bank[:, cols], m, 1, z_codes[:, cols], z_plane[:, cols])
+            nc.scalar.copy(out=head_result[:, m, :], in_=bank[:])
+            nc.sync.dma_start(out=out_rows[:, m, :HEAD], in_=head_result[:, m, :])
+
+        zt_words = sbuf([P, TAIL, PACK], BF16, "zt_words")
+        nc.vector.tensor_tensor(
+            out=zt_words[:], in0=pair_words[:], in1=late2[:].rearrange("p t v -> p v t"), op=MAX
+        )
+        zt_codes = sbuf([P, TAIL], U32, "zt_codes")
+        zt_plane = sbuf([P, TAIL], U8, "zt_plane")
+        quantise(zt_codes[:], zt_plane[:], zt_words[:])
+        tail_result = sbuf([P, 2, TAIL], F32, "tail_result")
+        for m in range(2):
+            product(tail_banks[m][:], m, 1, zt_codes[:], zt_plane[:])
+        nc.scalar.copy(out=tail_result[:, 0, :], in_=tail_banks[0][:])
+        nc.vector.tensor_copy(out=tail_result[:, 1, :], in_=tail_banks[1][:])
+        nc.sync.dma_start(out=out_rows[:, :, HEAD:], in_=tail_result[:])

@@ -17,9 +17,10 @@ RELU = mybir.ActivationFunctionType.Relu
 
 P = 128
 PACK = 4
-HEAD = 384
-TAIL = T - HEAD
-WINDOW = 2 * HEAD
+EARLY = 384
+WINDOW = 2 * EARLY
+LATE = 128
+RUN = 16
 M_VECTOR = 88
 
 
@@ -37,29 +38,34 @@ def tile_picked_wsagecat_max_l_kernel(
 
         x_plane = sbuf([P, T], U8, "x_plane")
         w_plane = sbuf([P, 2, N], U8, "w_plane")
-        nc.vector.memset(x_plane[:].bitcast(I32), 0)
+        nc.gpsimd.memset(x_plane[:].bitcast(I32), 0)
+        nc.gpsimd.memset(w_plane[:].rearrange("p i n -> p (i n)").bitcast(I32), 0)
 
         w1_rows = w1.rearrange("(g p j) c -> g p j c", g=2, j=PACK)
-        raw0 = sbuf([P, PACK, H], F32, "raw0")
-        raw1 = [sbuf([P, 2, H], F32, "raw1_%d" % u) for u in range(2)]
-        nc.sync.dma_start(out=raw0[:], in_=w1_rows[0])
+        raw = [[sbuf([P, PACK, P], F32, "raw%d_%d" % (c, g)) for g in range(2)] for c in range(4)]
+        lists = [lists_pool.tile([P, T // 16], U16, name="offsets%d" % d) for d in range(3)]
+
+        def load_w1(c):
+            for g in range(2):
+                nc.sync.dma_start(out=raw[c][g][:], in_=w1_rows[g][:, :, P * c : P * (c + 1)])
+
+        load_w1(0)
         for q in range(4):
             nc.sync.dma_start(
                 out=x_plane[32 * q : 32 * q + 8, :].bitcast(I32),
                 in_=x_scales[:, 4 * q : 4 * q + 4, :].bitcast(I32),
             )
-        for u in range(2):
-            nc.sync.dma_start(out=raw1[u][:], in_=w1_rows[1][:, 2 * u : 2 * u + 2, :])
-        x_codes = [sbuf([P, T], U32, "x_codes%d" % g) for g in range(2)]
+        x_codes = sbuf([P, 2, T], U32, "x_codes")
+        x_rows = x_words.rearrange("z p n r -> p z (n r)").bitcast(I32)
+        nc.sync.dma_start(out=x_codes[:, :, : T // 2].bitcast(I32), in_=x_rows[:, :, : T // 2])
         for g in range(2):
-            nc.sync.dma_start(
-                out=x_codes[g][:].bitcast(I32), in_=x_words[g].rearrange("p n r -> p (n r)").bitcast(I32)
-            )
-        lists = []
-        for d, pos in enumerate((pos1, pos2, pos3)):
-            offsets = lists_pool.tile([P, T // 16], U16, name="offsets%d" % d)
-            nc.sync.dma_start(offsets[:], pos)
-            lists.append(offsets)
+            nc.sync.dma_start(out=x_codes[:, g, T // 2 :].bitcast(I32), in_=x_rows[:, g, T // 2 :])
+        nc.sync.dma_start(lists[0][:], pos1)
+        nc.sync.dma_start(lists[1][:], pos2)
+        load_w1(1)
+        nc.sync.dma_start(lists[2][:], pos3)
+        load_w1(2)
+        load_w1(3)
         w_codes = []
         for i, words in enumerate((w2_words, w3_words)):
             codes = sbuf([P, N], U32, "w_codes%d" % i)
@@ -67,7 +73,6 @@ def tile_picked_wsagecat_max_l_kernel(
                 out=codes[:].bitcast(I32), in_=words[0].rearrange("p n r -> p (n r)").bitcast(I32)
             )
             w_codes.append(codes)
-        nc.vector.memset(w_plane[:].rearrange("p i n -> p (i n)").bitcast(I32), 0)
         for i, scales in enumerate((w2_scales, w3_scales)):
             for q in range(4):
                 nc.sync.dma_start(
@@ -75,113 +80,151 @@ def tile_picked_wsagecat_max_l_kernel(
                     in_=scales[0, 4 * q : 4 * q + 4, :].bitcast(I32),
                 )
 
-        windows = [sbuf([P, WINDOW], F32, "window%d" % t) for t in range(PACK)]
-        for t in range(PACK):
-            nc.vector.memset(windows[t][:, T:], 0.0)
-
-        w1_bf = [sbuf([P, PACK, P, PACK], BF16, "w1_bf%d" % g) for g in range(2)]
-        w1_codes = [sbuf([P, H], U32, "w1_codes%d" % g) for g in range(2)]
-        w1_plane = [sbuf([P, H], U8, "w1_plane%d" % g) for g in range(2)]
-
-        def cast(dst, src):
-            dst = dst.rearrange("p t m j -> p m j t")
-            src = src.rearrange("p j (m t) -> p m j t", t=PACK)
-            nc.vector.tensor_copy(out=dst[:, :M_VECTOR], in_=src[:, :M_VECTOR])
-            nc.scalar.copy(out=dst[:, M_VECTOR:], in_=src[:, M_VECTOR:])
-
-        def quantise_w1(g, t0, t1):
-            nc.vector.quantize_mx(
-                out=w1_codes[g][:, P * t0 : P * t1].bitcast(FP8X4),
-                scales=w1_plane[g][:, P * t0 : P * t1],
-                in_=w1_bf[g][:, t0:t1].rearrange("p t m j -> p (t m j)"),
-            )
-
-        cast(w1_bf[0][:], raw0[:])
-        quantise_w1(0, 0, 4)
-        for u in range(2):
-            cast(w1_bf[1][:, :, :, 2 * u : 2 * u + 2], raw1[u][:])
-        quantise_w1(1, 0, 1)
-        quantise_w1(1, 1, 2)
-        quantise_w1(1, 2, 4)
-
-        banks = [psum.tile([P, T], F32, name="h_bank%d" % t) for t in range(PACK)]
-        for t in range(PACK):
-            cols = slice(P * t, P * (t + 1))
-            for g in range(2):
-                nc.tensor.matmul_mx(
-                    out=banks[t][:],
-                    lhsT=w1_codes[g][:, cols].bitcast(FP8X4),
-                    lhsT_scale=w1_plane[g][:, cols],
-                    rhs=x_codes[g][:].bitcast(FP8X4),
-                    rhs_scale=x_plane[4 * g :, :],
-                    start=(g == 0),
-                    stop=(g == 1),
-                )
-            nc.scalar.activation(out=windows[t][:, :T], in_=banks[t][:], func=RELU)
+        def woven(dst, src):
+            return dst.rearrange("p (a i) t -> p a t i", i=4), src.rearrange("p t (a i) -> p a t i", i=4)
 
         def interleave(dst, src):
-            nc.scalar.copy(
-                out=dst.rearrange("p (c i) t -> p c t i", i=4),
-                in_=src.rearrange("p t (c i) -> p c t i", i=4),
-            )
-
-        h_rows = sbuf([P, PACK, T], BF16, "h_rows")
-        for t in range(PACK):
-            nc.scalar.activation(out=h_rows[:, t, :], in_=banks[t][:], func=RELU)
-        h_words = sbuf([P, T, PACK], BF16, "h_words", tag="reuse_h")
-        interleave(h_words[:], h_rows[:])
-
-        def gather(dst, t, d, v0, v1):
-            nc.vector.tensor_copy(out=dst, in_=windows[t][:].indirect(lists[d][:, v0 // 16 : v1 // 16]))
+            dst, src = woven(dst, src)
+            nc.scalar.copy(out=dst, in_=src)
 
         def quantise(codes, plane, words):
-            nc.vector.quantize_mx(
-                out=codes.bitcast(FP8X4), scales=plane, in_=words.rearrange("p v t -> p (v t)")
+            nc.vector.quantize_mx(out=codes.bitcast(FP8X4), scales=plane, in_=words)
+
+        w1_bf = [sbuf([P, 2, P, PACK], BF16, "w1_bf%d" % c) for c in range(4)]
+        w1_codes = [sbuf([P, 2 * P], U32, "w1_codes%d" % c) for c in range(4)]
+        w1_plane = [sbuf([P, 2 * P], U8, "w1_plane%d" % c) for c in range(4)]
+        windows = [sbuf([P, WINDOW], F32, "window%d" % c) for c in range(4)]
+        for c in range(4):
+            nc.gpsimd.memset(windows[c][:, T:], 0.0)
+        h_rows = sbuf([P, PACK, T], F32, "h_rows")
+        spans = [(0, 256), (256, EARLY - 256)]
+        z_rows = [sbuf([P, PACK, n], BF16, "z_rows%d" % v0) for v0, n in spans]
+
+        def first_product(bank, c, g, nodes):
+            cols = slice(P * g, P * (g + 1))
+            nc.tensor.matmul_mx(
+                out=bank,
+                lhsT=w1_codes[c][:, cols].bitcast(FP8X4),
+                lhsT_scale=w1_plane[c][:, cols],
+                rhs=x_codes[:, g, nodes].bitcast(FP8X4),
+                rhs_scale=x_plane[4 * g :, nodes],
+                start=(g == 0),
+                stop=(g == 1),
             )
 
-        picked = [sbuf([P, PACK, HEAD], BF16, "picked%d" % d) for d in range(3)]
-        z_rows = sbuf([P, PACK, HEAD], BF16, "z_rows")
+        for g in range(2):
+            dst, src = woven(w1_bf[0][:, g], raw[0][g][:])
+            nc.vector.tensor_copy(out=dst[:, : M_VECTOR // 4], in_=src[:, : M_VECTOR // 4])
+            nc.scalar.copy(out=dst[:, M_VECTOR // 4 :], in_=src[:, M_VECTOR // 4 :])
+        for g in range(2):
+            cols = slice(P * g, P * (g + 1))
+            quantise(w1_codes[0][:, cols], w1_plane[0][:, cols], w1_bf[0][:, g].rearrange("p m j -> p (m j)"))
+        pieces = [slice(0, 256), slice(256, 384), slice(384, 512)]
+        piece_banks = [
+            psum.tile([P, s.stop - s.start], F32, name="piece_bank%d" % u, tag="bank%d" % (0, 1, 7)[u])
+            for u, s in enumerate(pieces)
+        ]
+        for g in range(2):
+            first_product(piece_banks[0][:], 0, g, pieces[0])
+        for g in range(2):
+            for u in (1, 2):
+                first_product(piece_banks[u][:], 0, g, pieces[u])
+        for u in range(2):
+            nc.scalar.activation(out=windows[0][:, pieces[u]], in_=piece_banks[u][:], func=RELU)
+        nc.vector.tensor_scalar_max(out=windows[0][:, pieces[2]], in0=piece_banks[2][:], scalar1=0.0)
 
-        def first_max(ts):
-            nc.vector.tensor_tensor(out=z_rows[:, ts], in0=picked[0][:, ts], in1=picked[1][:, ts], op=MAX)
+        def make_window(c):
+            for g in range(2):
+                interleave(w1_bf[c][:, g], raw[c][g][:])
+            if c == 1:
+                for g in range(2):
+                    cols = slice(P * g, P * (g + 1))
+                    quantise(w1_codes[c][:, cols], w1_plane[c][:, cols], w1_bf[c][:, g].rearrange("p m j -> p (m j)"))
+            else:
+                quantise(w1_codes[c][:], w1_plane[c][:], w1_bf[c][:].rearrange("p g m j -> p (g m j)"))
+            bank = psum.tile([P, T], F32, name="h_bank%d" % c, tag="bank%d" % (c + 1))
+            for g in range(2):
+                first_product(bank[:], c, g, slice(0, T))
+            nc.scalar.activation(out=windows[c][:, :T], in_=bank[:], func=RELU)
 
-        def second_max(ts):
-            nc.vector.tensor_tensor(out=z_rows[:, ts], in0=z_rows[:, ts], in1=picked[2][:, ts], op=MAX)
+        def offsets(d, v0, n):
+            return lists[d][:, v0 // 16 : (v0 + n) // 16]
 
-        for t in range(2):
-            for d in range(3):
-                gather(picked[d][:, t, :], t, d, 0, HEAD)
-        gather(picked[0][:, 2, :], 2, 0, 0, HEAD)
-        first_max(slice(0, 2))
-        gather(picked[1][:, 2, :], 2, 1, 0, HEAD)
-        second_max(slice(0, 2))
-        gather(picked[2][:, 2, :], 2, 2, 0, HEAD)
+        def gather_early(dst, c, d, v0, n):
+            nc.vector.tensor_copy(out=dst, in_=windows[c][:].indirect(offsets(d, v0, n)))
+
+        def largest(dst, a, b):
+            nc.vector.tensor_tensor(out=dst, in0=a, in1=b, op=MAX)
+
+        def deal_window(c):
+            nc.sync.dma_start(out=h_rows[32 * c : 32 * (c + 1)], in_=windows[c][:, :T])
+
+        def deal_best(best, c):
+            for (v0, n), rows in zip(spans, z_rows):
+                nc.sync.dma_start(out=rows[32 * c : 32 * (c + 1)], in_=best[:, v0 : v0 + n])
+
+        deal_window(0)
+        picked = []
         for d in range(3):
-            gather(picked[d][:, 3, :], 3, d, 0, HEAD)
-        first_max(slice(2, 4))
+            if d == 2:
+                make_window(1)
+                deal_window(1)
+            picked.append(sbuf([P, EARLY], BF16, "picked0_%d" % d, "raw1_1" if d == 2 else None))
+            gather_early(picked[d][:], 0, d, 0, EARLY)
+        best = sbuf([P, EARLY], BF16, "best0")
+        largest(best[:], picked[0][:], picked[1][:])
+        largest(best[:], best[:], picked[2][:])
+        deal_best(best, 0)
+
+        picked = []
+        for d in range(3):
+            if d > 0:
+                make_window(d + 1)
+                deal_window(d + 1)
+            picked.append(sbuf([P, 2, EARLY], BF16, "picked12_%d" % d, "raw%d_1" % (d + 1) if d > 0 else None))
+            gather_early(picked[d][:, 0, :], 1, d, 0, EARLY)
+        for d in range(3):
+            gather_early(picked[d][:, 1, :], 2, d, 0, EARLY)
+        best = sbuf([P, 2, EARLY], BF16, "best12", "w1_codes3")
+        largest(best[:], picked[0][:], picked[1][:])
+        largest(best[:], best[:], picked[2][:])
+        for c in (1, 2):
+            deal_best(best[:, c - 1, :], c)
+
+        best = sbuf([P, EARLY], BF16, "best3")
+        picked = [sbuf([P, EARLY], BF16, "picked3_%d" % d) for d in range(3)]
+        for (v0, n), rows in zip(spans, z_rows):
+            cols = slice(v0, v0 + n)
+            for d in range(3):
+                gather_early(picked[d][:, cols], 3, d, v0, n)
+            largest(best[:, cols], picked[0][:, cols], picked[1][:, cols])
+            largest(best[:, cols], best[:, cols], picked[2][:, cols])
+            nc.sync.dma_start(out=rows[96:], in_=best[:, cols])
+
+        h_words = sbuf([P, T, PACK], BF16, "h_words")
+        interleave(h_words[:], h_rows[:])
+        z_words = [sbuf([P, n, PACK], BF16, "z_words%d" % v0) for v0, n in spans]
+        for words, rows in zip(z_words, z_rows):
+            interleave(words[:], rows[:])
+
+        def gather_late(dst, d, v0):
+            for t in range(PACK):
+                nc.vector.tensor_copy(out=dst[:, :, t, :], in_=h_rows[:, t, :].indirect(offsets(d, v0, LATE)))
+
+        def late_tile(name, tag=None):
+            return sbuf([P, LATE // RUN, PACK, RUN], BF16, name, tag)
+
+        def words_of(dst, src):
+            nc.scalar.copy(out=dst[:].rearrange("p (a i) t -> p a i t", i=RUN), in_=src[:].rearrange("p a t i -> p a i t"))
+
+        last = EARLY
+        late0 = late_tile("late0")
+        gather_late(late0, 0, last)
+        late1 = late_tile("late1")
+        gather_late(late1, 1, last)
         h_codes = sbuf([P, T], U32, "h_codes")
         h_plane = sbuf([P, T], U8, "h_plane")
-        quantise(h_codes[:], h_plane[:], h_words[:])
-        second_max(slice(2, 4))
-        z_words = sbuf([P, HEAD, PACK], BF16, "z_words", tag="reuse_z")
-        interleave(z_words[:], z_rows[:])
-
-        late0 = sbuf([P, PACK, TAIL], BF16, "late0", tag="reuse_h")
-        late1 = sbuf([P, PACK, TAIL], BF16, "late1")
-        for d, dst in enumerate((late0, late1)):
-            for t in range(PACK):
-                gather(dst[:, t, :], t, d, HEAD, T)
-        z_codes = sbuf([P, HEAD], U32, "z_codes")
-        z_plane = sbuf([P, HEAD], U8, "z_plane")
-        quantise(z_codes[:, :256], z_plane[:, :256], z_words[:, :256, :])
-        pair_rows = sbuf([P, PACK, TAIL], BF16, "pair_rows")
-        nc.vector.tensor_tensor(out=pair_rows[:], in0=late0[:], in1=late1[:], op=MAX)
-        quantise(z_codes[:, 256:], z_plane[:, 256:], z_words[:, 256:, :])
-        pair_words = sbuf([P, TAIL, PACK], BF16, "pair_words")
-        interleave(pair_words[:], pair_rows[:])
-        late2 = sbuf([P, PACK, TAIL], BF16, "late2", tag="reuse_z")
-        for t in range(PACK):
-            gather(late2[:, t, :], t, 2, HEAD, T)
+        quantise(h_codes[:], h_plane[:], h_words[:].rearrange("p v t -> p (v t)"))
 
         def product(bank, m, i, codes, plane):
             cols = slice(P * m, P * (m + 1))
@@ -196,28 +239,48 @@ def tile_picked_wsagecat_max_l_kernel(
             )
 
         out_rows = out.rearrange("(m p) v -> p m v", p=P)
-        tail_banks = [psum.tile([P, TAIL], F32, name="tail_bank%d" % m) for m in range(2)]
+        last_banks = [psum.tile([P, LATE], F32, name="last_bank%d" % m, tag="bank%d" % (5 + m)) for m in range(2)]
         for m in range(2):
-            product(tail_banks[m][:], m, 0, h_codes[:, HEAD:], h_plane[:, HEAD:])
-        head_result = sbuf([P, 2, HEAD], F32, "head_result")
-        for m in range(2):
-            bank = psum.tile([P, HEAD], F32, name="head_bank%d" % m)
-            for cols in (slice(0, 256), slice(256, HEAD)):
-                product(bank[:, cols], m, 0, h_codes[:, cols], h_plane[:, cols])
-                product(bank[:, cols], m, 1, z_codes[:, cols], z_plane[:, cols])
-            nc.scalar.copy(out=head_result[:, m, :], in_=bank[:])
-            nc.sync.dma_start(out=out_rows[:, m, :HEAD], in_=head_result[:, m, :])
+            product(last_banks[m][:], m, 0, h_codes[:, last:], h_plane[:, last:])
 
-        zt_words = sbuf([P, TAIL, PACK], BF16, "zt_words")
+        def finish(words, v0, n, tag):
+            codes = sbuf([P, n], U32, "z_codes%d" % v0)
+            plane = sbuf([P, n], U8, "z_plane%d" % v0)
+            quantise(codes[:], plane[:], words[:].rearrange("p v t -> p (v t)"))
+            bank = psum.tile([P, 2, n], F32, name="out_bank%d" % v0, tag=tag)
+            for m in range(2):
+                product(bank[:, m, :], m, 0, h_codes[:, v0 : v0 + n], h_plane[:, v0 : v0 + n])
+                product(bank[:, m, :], m, 1, codes[:], plane[:])
+            return bank
+
+        def store(bank, v0, n):
+            result = sbuf([P, 2, n], F32, "result%d" % v0)
+            nc.scalar.copy(out=result[:], in_=bank[:])
+            nc.sync.dma_start(out=out_rows[:, :, v0 : v0 + n], in_=result[:])
+
+        pair = late_tile("pair", "z_rows0")
+        largest(pair[:], late0[:], late1[:])
+        pair_words = sbuf([P, LATE, PACK], BF16, "pair_words")
+        words_of(pair_words, pair)
+        banks = [finish(words, v0, n, "bank%d" % u) for u, ((v0, n), words) in enumerate(zip(spans, z_words))]
+        late2 = late_tile("late2", "z_rows256")
+        gather_late(late2, 2, last)
+        for (v0, n), bank in zip(spans, banks):
+            store(bank, v0, n)
+
+        z2_words = sbuf([P, LATE, PACK], BF16, "z2_words")
         nc.vector.tensor_tensor(
-            out=zt_words[:], in0=pair_words[:], in1=late2[:].rearrange("p t v -> p v t"), op=MAX
+            out=z2_words[:].rearrange("p (a i) t -> p a i t", i=RUN),
+            in0=pair_words[:].rearrange("p (a i) t -> p a i t", i=RUN),
+            in1=late2[:].rearrange("p a t i -> p a i t"),
+            op=MAX,
         )
-        zt_codes = sbuf([P, TAIL], U32, "zt_codes")
-        zt_plane = sbuf([P, TAIL], U8, "zt_plane")
-        quantise(zt_codes[:], zt_plane[:], zt_words[:])
-        tail_result = sbuf([P, 2, TAIL], F32, "tail_result")
+        z2_codes = sbuf([P, LATE], U32, "z2_codes")
+        z2_plane = sbuf([P, LATE], U8, "z2_plane")
+        quantise(z2_codes[:], z2_plane[:], z2_words[:].rearrange("p v t -> p (v t)"))
+        last_result = sbuf([P, 2, LATE], F32, "last_result")
         for m in range(2):
-            product(tail_banks[m][:], m, 1, zt_codes[:], zt_plane[:])
-        nc.scalar.copy(out=tail_result[:, 0, :], in_=tail_banks[0][:])
-        nc.vector.tensor_copy(out=tail_result[:, 1, :], in_=tail_banks[1][:])
-        nc.sync.dma_start(out=out_rows[:, :, HEAD:], in_=tail_result[:])
+            product(last_banks[m][:], m, 1, z2_codes[:], z2_plane[:])
+        nc.scalar.copy(out=last_result[:, 0, :], in_=last_banks[0][:])
+        nc.vector.tensor_copy(out=last_result[:, 1, :], in_=last_banks[1][:])
+        nc.sync.dma_start(out=out_rows[:, :, last:], in_=last_result[:])

@@ -20,7 +20,6 @@ PACK = 4
 EARLY = 384
 WINDOW = 2 * EARLY
 LATE = 128
-RUN = 16
 M_VECTOR = 88
 
 
@@ -45,16 +44,17 @@ def tile_picked_wsagecat_max_l_kernel(
         raw = [[sbuf([P, PACK, P], F32, "raw%d_%d" % (c, g)) for g in range(2)] for c in range(4)]
         lists = [lists_pool.tile([P, T // 16], U16, name="offsets%d" % d) for d in range(3)]
 
-        def load_w1(c):
-            for g in range(2):
+        def load_w1(c, passes=(0, 1)):
+            for g in passes:
                 nc.sync.dma_start(out=raw[c][g][:], in_=w1_rows[g][:, :, P * c : P * (c + 1)])
 
-        load_w1(0)
+        load_w1(0, (0,))
         for q in range(4):
             nc.sync.dma_start(
                 out=x_plane[32 * q : 32 * q + 8, :].bitcast(I32),
                 in_=x_scales[:, 4 * q : 4 * q + 4, :].bitcast(I32),
             )
+        load_w1(0, (1,))
         x_codes = sbuf([P, 2, T], U32, "x_codes")
         x_rows = x_words.rearrange("z p n r -> p z (n r)").bitcast(I32)
         nc.sync.dma_start(out=x_codes[:, :, : T // 2].bitcast(I32), in_=x_rows[:, :, : T // 2])
@@ -209,13 +209,10 @@ def tile_picked_wsagecat_max_l_kernel(
 
         def gather_late(dst, d, v0):
             for t in range(PACK):
-                nc.vector.tensor_copy(out=dst[:, :, t, :], in_=h_rows[:, t, :].indirect(offsets(d, v0, LATE)))
+                nc.vector.tensor_copy(out=dst[:, t, :], in_=h_rows[:, t, :].indirect(offsets(d, v0, LATE)))
 
-        def late_tile(name, tag=None):
-            return sbuf([P, LATE // RUN, PACK, RUN], BF16, name, tag)
-
-        def words_of(dst, src):
-            nc.scalar.copy(out=dst[:].rearrange("p (a i) t -> p a i t", i=RUN), in_=src[:].rearrange("p a t i -> p a i t"))
+        def late_tile(name, tag=None, dtype=F32):
+            return sbuf([P, PACK, LATE], dtype, name, tag)
 
         last = EARLY
         late0 = late_tile("late0")
@@ -258,10 +255,10 @@ def tile_picked_wsagecat_max_l_kernel(
             nc.scalar.copy(out=result[:], in_=bank[:])
             nc.sync.dma_start(out=out_rows[:, :, v0 : v0 + n], in_=result[:])
 
-        pair = late_tile("pair", "z_rows0")
+        pair = late_tile("pair", "z_rows0", BF16)
         largest(pair[:], late0[:], late1[:])
         pair_words = sbuf([P, LATE, PACK], BF16, "pair_words")
-        words_of(pair_words, pair)
+        interleave(pair_words[:], pair[:])
         banks = [finish(words, v0, n, "bank%d" % u) for u, ((v0, n), words) in enumerate(zip(spans, z_words))]
         late2 = late_tile("late2", "z_rows256")
         gather_late(late2, 2, last)
@@ -270,9 +267,9 @@ def tile_picked_wsagecat_max_l_kernel(
 
         z2_words = sbuf([P, LATE, PACK], BF16, "z2_words")
         nc.vector.tensor_tensor(
-            out=z2_words[:].rearrange("p (a i) t -> p a i t", i=RUN),
-            in0=pair_words[:].rearrange("p (a i) t -> p a i t", i=RUN),
-            in1=late2[:].rearrange("p a t i -> p a i t"),
+            out=z2_words[:],
+            in0=pair_words[:],
+            in1=late2[:].rearrange("p t v -> p v t"),
             op=MAX,
         )
         z2_codes = sbuf([P, LATE], U32, "z2_codes")

@@ -37,8 +37,8 @@ def tile_picked_wsagecat_max_l_kernel(
 
         x_plane = sbuf([P, T], U8, "x_plane")
         w_plane = sbuf([P, 2, N], U8, "w_plane")
-        nc.gpsimd.memset(x_plane[:].bitcast(I32), 0)
-        nc.gpsimd.memset(w_plane[:].rearrange("p i n -> p (i n)").bitcast(I32), 0)
+        nc.vector.memset(x_plane[:].bitcast(I32), 0)
+        nc.vector.memset(w_plane[:].rearrange("p i n -> p (i n)").bitcast(I32), 0)
 
         w1_rows = w1.rearrange("(g p j) c -> g p j c", g=2, j=PACK)
         raw = [[sbuf([P, PACK, P], F32, "raw%d_%d" % (c, g)) for g in range(2)] for c in range(4)]
@@ -61,8 +61,9 @@ def tile_picked_wsagecat_max_l_kernel(
         for g in range(2):
             nc.sync.dma_start(out=x_codes[:, g, T // 2 :].bitcast(I32), in_=x_rows[:, g, T // 2 :])
         nc.sync.dma_start(lists[0][:], pos1)
+        load_w1(1, (0,))
         nc.sync.dma_start(lists[1][:], pos2)
-        load_w1(1)
+        load_w1(1, (1,))
         nc.sync.dma_start(lists[2][:], pos3)
         load_w1(2)
         load_w1(3)
@@ -95,7 +96,7 @@ def tile_picked_wsagecat_max_l_kernel(
         w1_plane = [sbuf([P, 2 * P], U8, "w1_plane%d" % c) for c in range(4)]
         windows = [sbuf([P, WINDOW], F32, "window%d" % c) for c in range(4)]
         for c in range(4):
-            nc.gpsimd.memset(windows[c][:, T:], 0.0)
+            nc.vector.memset(windows[c][:, T:], 0.0)
         h_rows = sbuf([P, PACK, T], F32, "h_rows")
         spans = [(0, 256), (256, EARLY - 256)]
         z_rows = [sbuf([P, PACK, n], BF16, "z_rows%d" % v0) for v0, n in spans]
@@ -142,10 +143,15 @@ def tile_picked_wsagecat_max_l_kernel(
                     quantise(w1_codes[c][:, cols], w1_plane[c][:, cols], w1_bf[c][:, g].rearrange("p m j -> p (m j)"))
             else:
                 quantise(w1_codes[c][:], w1_plane[c][:], w1_bf[c][:].rearrange("p g m j -> p (g m j)"))
-            bank = psum.tile([P, T], F32, name="h_bank%d" % c, tag="bank%d" % (c + 1))
+            halves = [slice(0, T // 2), slice(T // 2, T)]
+            banks = [
+                psum.tile([P, T // 2], F32, name="h_bank%d_%d" % (c, u), tag="bank%d" % (2 * c + u)) for u in range(2)
+            ]
             for g in range(2):
-                first_product(bank[:], c, g, slice(0, T))
-            nc.scalar.activation(out=windows[c][:, :T], in_=bank[:], func=RELU)
+                for u in range(2):
+                    first_product(banks[u][:], c, g, halves[u])
+            for u in range(2):
+                nc.scalar.activation(out=windows[c][:, halves[u]], in_=banks[u][:], func=RELU)
 
         def offsets(d, v0, n):
             return lists[d][:, v0 // 16 : (v0 + n) // 16]
@@ -166,12 +172,12 @@ def tile_picked_wsagecat_max_l_kernel(
         deal_window(0)
         picked = []
         for d in range(3):
-            if d == 2:
+            if d == 1:
                 make_window(1)
                 deal_window(1)
-            picked.append(sbuf([P, EARLY], BF16, "picked0_%d" % d, "raw1_1" if d == 2 else None))
+            picked.append(sbuf([P, EARLY], BF16, "picked0_%d" % d, "raw1_%d" % (d - 1) if d > 0 else None))
             gather_early(picked[d][:], 0, d, 0, EARLY)
-        best = sbuf([P, EARLY], BF16, "best0")
+        best = sbuf([P, EARLY], BF16, "best0", "w1_bf1")
         largest(best[:], picked[0][:], picked[1][:])
         largest(best[:], best[:], picked[2][:])
         deal_best(best, 0)

from contextlib import ExitStack

import concourse.mybir as mybir

K, T, H, N = 1024, 512, 512, 256
FLOPS = 2 * K * H * T + 2 * 2 * H * N * T

F32 = mybir.dt.float32
BF16 = mybir.dt.bfloat16
I32 = mybir.dt.int32
U32 = mybir.dt.uint32
U16 = mybir.dt.uint16
U8 = mybir.dt.uint8
FP8X4 = mybir.dt.float8_e4m3fn_x4
MAX = mybir.AluOpType.max
RELU = mybir.ActivationFunctionType.Relu

P = 128
PACK = 4
EARLY = 384
WINDOW = 2 * EARLY
LATE = 128
M_VECTOR = 88


def tile_picked_wsagecat_max_l_kernel(
    tc, x_words, x_scales, w1, w2_words, w2_scales, w3_words, w3_scales, pos1, pos2, pos3, out
):
    nc = tc.nc
    with ExitStack() as ctx:
        lists_pool = ctx.enter_context(tc.tile_pool(name="lists", bufs=1))
        keep = ctx.enter_context(tc.tile_pool(name="keep", bufs=1))
        psum = ctx.enter_context(tc.psum_pool(name="psum", bufs=1))

        def sbuf(shape, dtype, name, tag=None):
            return keep.tile(shape, dtype, name=name, tag=tag or name, align_bytes=64)

        x_plane = sbuf([P, T], U8, "x_plane")
        w_plane = sbuf([P, 2, N], U8, "w_plane")
        nc.vector.memset(x_plane[:].bitcast(I32), 0)
        nc.vector.memset(w_plane[:].rearrange("p i n -> p (i n)").bitcast(I32), 0)

        w1_rows = w1.rearrange("(g p j) c -> g p j c", g=2, j=PACK)
        raw = [[sbuf([P, PACK, P], F32, "raw%d_%d" % (c, g)) for g in range(2)] for c in range(4)]
        lists = [lists_pool.tile([P, T // 16], U16, name="offsets%d" % d) for d in range(3)]

        def load_w1(c, passes=(0, 1)):
            for g in passes:
                nc.sync.dma_start(out=raw[c][g][:], in_=w1_rows[g][:, :, P * c : P * (c + 1)])

        load_w1(0, (0,))
        for q in range(4):
            nc.sync.dma_start(
                out=x_plane[32 * q : 32 * q + 8, :].bitcast(I32),
                in_=x_scales[:, 4 * q : 4 * q + 4, :].bitcast(I32),
            )
        load_w1(0, (1,))
        x_codes = sbuf([P, 2, T], U32, "x_codes")
        x_rows = x_words.rearrange("z p n r -> p z (n r)").bitcast(I32)
        nc.sync.dma_start(out=x_codes[:, :, : T // 2].bitcast(I32), in_=x_rows[:, :, : T // 2])
        for g in range(2):
            nc.sync.dma_start(out=x_codes[:, g, T // 2 :].bitcast(I32), in_=x_rows[:, g, T // 2 :])
        nc.sync.dma_start(lists[0][:], pos1)
        load_w1(1, (0,))
        nc.sync.dma_start(lists[1][:], pos2)
        load_w1(1, (1,))
        nc.sync.dma_start(lists[2][:], pos3)
        load_w1(2)
        load_w1(3)
        w_codes = []
        for i, words in enumerate((w2_words, w3_words)):
            codes = sbuf([P, N], U32, "w_codes%d" % i)
            nc.sync.dma_start(
                out=codes[:].bitcast(I32), in_=words[0].rearrange("p n r -> p (n r)").bitcast(I32)
            )
            w_codes.append(codes)
        for i, scales in enumerate((w2_scales, w3_scales)):
            for q in range(4):
                nc.sync.dma_start(
                    out=w_plane[32 * q : 32 * q + 4, i, :].bitcast(I32),
                    in_=scales[0, 4 * q : 4 * q + 4, :].bitcast(I32),
                )

        def woven(dst, src):
            return dst.rearrange("p (a i) t -> p a t i", i=4), src.rearrange("p t (a i) -> p a t i", i=4)

        def interleave(dst, src):
            dst, src = woven(dst, src)
            nc.scalar.copy(out=dst, in_=src)

        def quantise(codes, plane, words):
            nc.vector.quantize_mx(out=codes.bitcast(FP8X4), scales=plane, in_=words)

        w1_bf = [sbuf([P, 2, P, PACK], BF16, "w1_bf%d" % c) for c in range(4)]
        w1_codes = [sbuf([P, 2 * P], U32, "w1_codes%d" % c) for c in range(4)]
        w1_plane = [sbuf([P, 2 * P], U8, "w1_plane%d" % c) for c in range(4)]
        windows = [sbuf([P, WINDOW], F32, "window%d" % c) for c in range(4)]
        for c in range(4):
            nc.vector.memset(windows[c][:, T:], 0.0)
        h_rows = sbuf([P, PACK, T], F32, "h_rows")
        spans = [(0, 256), (256, EARLY - 256)]
        z_rows = [sbuf([P, PACK, n], BF16, "z_rows%d" % v0) for v0, n in spans]

        def first_product(bank, c, g, nodes):
            cols = slice(P * g, P * (g + 1))
            nc.tensor.matmul_mx(
                out=bank,
                lhsT=w1_codes[c][:, cols].bitcast(FP8X4),
                lhsT_scale=w1_plane[c][:, cols],
                rhs=x_codes[:, g, nodes].bitcast(FP8X4),
                rhs_scale=x_plane[4 * g :, nodes],
                start=(g == 0),
                stop=(g == 1),
            )

        for g in range(2):
            dst, src = woven(w1_bf[0][:, g], raw[0][g][:])
            nc.vector.tensor_copy(out=dst[:, : M_VECTOR // 4], in_=src[:, : M_VECTOR // 4])
            nc.scalar.copy(out=dst[:, M_VECTOR // 4 :], in_=src[:, M_VECTOR // 4 :])
        for g in range(2):
            cols = slice(P * g, P * (g + 1))
            quantise(w1_codes[0][:, cols], w1_plane[0][:, cols], w1_bf[0][:, g].rearrange("p m j -> p (m j)"))
        pieces = [slice(0, 256), slice(256, 384), slice(384, 512)]
        piece_banks = [
            psum.tile([P, s.stop - s.start], F32, name="piece_bank%d" % u, tag="bank%d" % (0, 1, 7)[u])
            for u, s in enumerate(pieces)
        ]
        for g in range(2):
            first_product(piece_banks[0][:], 0, g, pieces[0])
        for g in range(2):
            for u in (1, 2):
                first_product(piece_banks[u][:], 0, g, pieces[u])
        for u in range(2):
            nc.scalar.activation(out=windows[0][:, pieces[u]], in_=piece_banks[u][:], func=RELU)
        nc.vector.tensor_scalar_max(out=windows[0][:, pieces[2]], in0=piece_banks[2][:], scalar1=0.0)

        def make_window(c):
            for g in range(2):
                interleave(w1_bf[c][:, g], raw[c][g][:])
            if c == 1:
                for g in range(2):
                    cols = slice(P * g, P * (g + 1))
                    quantise(w1_codes[c][:, cols], w1_plane[c][:, cols], w1_bf[c][:, g].rearrange("p m j -> p (m j)"))
            else:
                quantise(w1_codes[c][:], w1_plane[c][:], w1_bf[c][:].rearrange("p g m j -> p (g m j)"))
            halves = [slice(0, T // 2), slice(T // 2, T)]
            banks = [
                psum.tile([P, T // 2], F32, name="h_bank%d_%d" % (c, u), tag="bank%d" % (2 * c + u)) for u in range(2)
            ]
            for g in range(2):
                for u in range(2):
                    first_product(banks[u][:], c, g, halves[u])
            for u in range(2):
                nc.scalar.activation(out=windows[c][:, halves[u]], in_=banks[u][:], func=RELU)

        def offsets(d, v0, n):
            return lists[d][:, v0 // 16 : (v0 + n) // 16]

        def gather_early(dst, c, d, v0, n):
            nc.vector.tensor_copy(out=dst, in_=windows[c][:].indirect(offsets(d, v0, n)))

        def largest(dst, a, b):
            nc.vector.tensor_tensor(out=dst, in0=a, in1=b, op=MAX)

        def deal_window(c):
            nc.sync.dma_start(out=h_rows[32 * c : 32 * (c + 1)], in_=windows[c][:, :T])

        def deal_best(best, c):
            for (v0, n), rows in zip(spans, z_rows):
                nc.sync.dma_start(out=rows[32 * c : 32 * (c + 1)], in_=best[:, v0 : v0 + n])

        deal_window(0)
        picked = []
        for d in range(3):
            if d == 1:
                make_window(1)
                deal_window(1)
            picked.append(sbuf([P, EARLY], BF16, "picked0_%d" % d, "raw1_%d" % (d - 1) if d > 0 else None))
            gather_early(picked[d][:], 0, d, 0, EARLY)
        best = sbuf([P, EARLY], BF16, "best0", "w1_bf1")
        largest(best[:], picked[0][:], picked[1][:])
        largest(best[:], best[:], picked[2][:])
        deal_best(best, 0)

        picked = []
        for d in range(3):
            if d > 0:
                make_window(d + 1)
                deal_window(d + 1)
            picked.append(sbuf([P, 2, EARLY], BF16, "picked12_%d" % d, "raw%d_1" % (d + 1) if d > 0 else None))
            gather_early(picked[d][:, 0, :], 1, d, 0, EARLY)
        for d in range(3):
            gather_early(picked[d][:, 1, :], 2, d, 0, EARLY)
        best = sbuf([P, 2, EARLY], BF16, "best12", "w1_codes3")
        largest(best[:], picked[0][:], picked[1][:])
        largest(best[:], best[:], picked[2][:])
        for c in (1, 2):
            deal_best(best[:, c - 1, :], c)

        best = sbuf([P, EARLY], BF16, "best3")
        picked = [sbuf([P, EARLY], BF16, "picked3_%d" % d) for d in range(3)]
        for (v0, n), rows in zip(spans, z_rows):
            cols = slice(v0, v0 + n)
            for d in range(3):
                gather_early(picked[d][:, cols], 3, d, v0, n)
            largest(best[:, cols], picked[0][:, cols], picked[1][:, cols])
            largest(best[:, cols], best[:, cols], picked[2][:, cols])
            nc.sync.dma_start(out=rows[96:], in_=best[:, cols])

        h_words = sbuf([P, T, PACK], BF16, "h_words")
        interleave(h_words[:], h_rows[:])
        z_words = [sbuf([P, n, PACK], BF16, "z_words%d" % v0) for v0, n in spans]
        for words, rows in zip(z_words, z_rows):
            interleave(words[:], rows[:])

        def gather_late(dst, d, v0):
            for t in range(PACK):
                nc.vector.tensor_copy(out=dst[:, t, :], in_=h_rows[:, t, :].indirect(offsets(d, v0, LATE)))

        def late_tile(name, tag=None, dtype=F32):
            return sbuf([P, PACK, LATE], dtype, name, tag)

        last = EARLY
        late0 = late_tile("late0")
        gather_late(late0, 0, last)
        late1 = late_tile("late1")
        gather_late(late1, 1, last)
        h_codes = sbuf([P, T], U32, "h_codes")
        h_plane = sbuf([P, T], U8, "h_plane")
        quantise(h_codes[:], h_plane[:], h_words[:].rearrange("p v t -> p (v t)"))

        def product(bank, m, i, codes, plane):
            cols = slice(P * m, P * (m + 1))
            nc.tensor.matmul_mx(
                out=bank,
                lhsT=w_codes[i][:, cols].bitcast(FP8X4),
                lhsT_scale=w_plane[:, i, cols],
                rhs=codes.bitcast(FP8X4),
                rhs_scale=plane,
                start=(i == 0),
                stop=(i == 1),
            )

        out_rows = out.rearrange("(m p) v -> p m v", p=P)
        last_banks = [psum.tile([P, LATE], F32, name="last_bank%d" % m, tag="bank%d" % (5 + m)) for m in range(2)]
        for m in range(2):
            product(last_banks[m][:], m, 0, h_codes[:, last:], h_plane[:, last:])

        def finish(words, v0, n, tag):
            codes = sbuf([P, n], U32, "z_codes%d" % v0)
            plane = sbuf([P, n], U8, "z_plane%d" % v0)
            quantise(codes[:], plane[:], words[:].rearrange("p v t -> p (v t)"))
            bank = psum.tile([P, 2, n], F32, name="out_bank%d" % v0, tag=tag)
            for m in range(2):
                product(bank[:, m, :], m, 0, h_codes[:, v0 : v0 + n], h_plane[:, v0 : v0 + n])
                product(bank[:, m, :], m, 1, codes[:], plane[:])
            return bank

        def store(bank, v0, n):
            result = sbuf([P, 2, n], F32, "result%d" % v0)
            nc.scalar.copy(out=result[:], in_=bank[:])
            nc.sync.dma_start(out=out_rows[:, :, v0 : v0 + n], in_=result[:])

        pair = late_tile("pair", "z_rows0", BF16)
        largest(pair[:], late0[:], late1[:])
        pair_words = sbuf([P, LATE, PACK], BF16, "pair_words")
        interleave(pair_words[:], pair[:])
        banks = [finish(words, v0, n, "bank%d" % u) for u, ((v0, n), words) in enumerate(zip(spans, z_words))]
        late2 = late_tile("late2", "z_rows256")
        gather_late(late2, 2, last)
        for (v0, n), bank in zip(spans, banks):
            store(bank, v0, n)

        z2_words = sbuf([P, LATE, PACK], BF16, "z2_words")
        nc.vector.tensor_tensor(
            out=z2_words[:],
            in0=pair_words[:],
            in1=late2[:].rearrange("p t v -> p v t"),
            op=MAX,
        )
        z2_codes = sbuf([P, LATE], U32, "z2_codes")
        z2_plane = sbuf([P, LATE], U8, "z2_plane")
        quantise(z2_codes[:], z2_plane[:], z2_words[:].rearrange("p v t -> p (v t)"))
        last_result = sbuf([P, 2, LATE], F32, "last_result")
        for m in range(2):
            product(last_banks[m][:], m, 1, z2_codes[:], z2_plane[:])
        nc.scalar.copy(out=last_result[:, 0, :], in_=last_banks[0][:])
        nc.vector.tensor_copy(out=last_result[:, 1, :], in_=last_banks[1][:])
        nc.sync.dma_start(out=out_rows[:, :, last:], in_=last_result[:])
